import numpy as np
CORES = [7,135,263,391,15,143,271,399,23,151,279,407,31,159,287,415]
N = 16
PERM = [[0,4],[1,5],[2,6],[3,7],[4,8],[5,9],[6,10],[7,11],[8,12],[9,13],[10,14],[11,15],[12,0],[13,1],[14,2],[15,3]]
def setup_inputs(rng):
    return {"x": rng.standard_normal((N, 128, 1024), dtype=np.float32)}
def reference(x):
    y = np.empty_like(x)
    for s, d in PERM:
        y[d] = x[s]
    return {"y": y}

@@ -1,0 +1,23 @@
+SCRATCH = {
+    "stage": ("sbuf", [128, 1024], "float32"),
+    "land": ("sbuf", [128, 1024], "float32"),
+}
+SEMAPHORES = ["loaded", "sent", "arrived", "stored"]
+
+
+def rank_program(g, core, T, topo):
+    rank = T.rank_of(core)
+    if rank is None:
+        return
+    dst = None
+    for s, d in T.tables["PERM"]:
+        if s == rank:
+            dst = T.cores[d]
+    g.sync.dma_start(T.stage[:], T.x[:]).then_inc(T.sem.loaded, 16)
+    g.wait_ge(T.sem.loaded, 16)
+    rid, pid = topo.addr(dst, core)
+    g.remote_dma(T.land[:], T.stage[:], T.sem.arrived, T.sem.sent, pid, rid, topo.mask(core, dst))
+    g.scalar.wait_ge(T.sem.arrived, 8)
+    g.scalar.dma_start(T.y[:], T.land[:]).then_inc(T.sem.stored, 16)
+    g.wait_ge(T.sem.sent, 8)
+    g.wait_ge(T.sem.stored, 16)

@@ -1,23 +1,71 @@
+NCHUNK = 4
+ROWS = 128 // NCHUNK
+COLS = 1024 // (128 // ROWS)
+
 SCRATCH = {
-    "stage": ("sbuf", [128, 1024], "float32"),
-    "land": ("sbuf", [128, 1024], "float32"),
+    "stage": ("dram", [NCHUNK, 128, COLS], "float32"),
+    "land": ("dram", [NCHUNK, 128, COLS], "float32"),
 }
-SEMAPHORES = ["loaded", "sent", "arrived", "stored"]
+SEMAPHORES = (["ld%d" % k for k in range(NCHUNK)]
+              + ["rel%d" % k for k in range(NCHUNK)]
+              + ["arr%d" % k for k in range(NCHUNK)]
+              + ["sent", "stored"])
+
+
+def _engines(mask):
+    return bin(mask).count("1")
+
+
+def _helper(topo, src, dst):
+    base = src - src % 8
+    for c in range(base + 7, base - 1, -1):
+        if topo.die(c) != topo.die(src) and topo.may_write(c, dst):
+            return c
+    return None
 
 
 def rank_program(g, core, T, topo):
+    routes = [(T.cores[s], T.cores[d]) for s, d in T.tables["PERM"]]
     rank = T.rank_of(core)
+
     if rank is None:
+        for src, dst in routes:
+            if _helper(topo, src, dst) != core:
+                continue
+            rid, pid = topo.addr(dst, core)
+            mask = topo.mask(core, dst)
+            left = 0
+            for k in range(0, NCHUNK, 2):
+                g.wait_ge(T.sem["rel%d" % k], _engines(topo.mask(src, core)))
+                g.remote_dma(T.land[k], T.stage[k], T.sem["arr%d" % k], T.sem.sent, pid, rid, mask)
+                left += _engines(mask)
+            g.wait_ge(T.sem.sent, left)
         return
-    dst = None
-    for s, d in T.tables["PERM"]:
-        if s == rank:
-            dst = T.cores[d]
-    g.sync.dma_start(T.stage[:], T.x[:]).then_inc(T.sem.loaded, 16)
-    g.wait_ge(T.sem.loaded, 16)
-    rid, pid = topo.addr(dst, core)
-    g.remote_dma(T.land[:], T.stage[:], T.sem.arrived, T.sem.sent, pid, rid, topo.mask(core, dst))
-    g.scalar.wait_ge(T.sem.arrived, 8)
-    g.scalar.dma_start(T.y[:], T.land[:]).then_inc(T.sem.stored, 16)
-    g.wait_ge(T.sem.sent, 8)
-    g.wait_ge(T.sem.stored, 16)
+
+    dst = [d for s, d in routes if s == core][0]
+    src = [s for s, d in routes if d == core][0]
+    helper = _helper(topo, core, dst)
+
+    for k in range(NCHUNK):
+        g.sync.dma_start(T.stage[k], T.x[k * ROWS:(k + 1) * ROWS, :]).then_inc(T.sem["ld%d" % k], 16)
+
+    left = 0
+    for k in range(NCHUNK):
+        g.wait_ge(T.sem["ld%d" % k], 16)
+        if k % 2 == 0:
+            to, out, sem = helper, T.stage[k], T.sem["rel%d" % k]
+        else:
+            to, out, sem = dst, T.land[k], T.sem["arr%d" % k]
+        rid, pid = topo.addr(to, core)
+        mask = topo.mask(core, to)
+        g.remote_dma(out, T.stage[k], sem, T.sem.sent, pid, rid, mask)
+        left += _engines(mask)
+
+    for k in range(NCHUNK):
+        q = g.sync if k % 2 == 0 else g.scalar
+        frm = _helper(topo, src, core) if k % 2 == 0 else src
+        q.wait_ge(T.sem["arr%d" % k], _engines(topo.mask(frm, core)))
+        q.dma_start(T.y[k * ROWS:(k + 1) * ROWS, :], T.land[k]).then_inc(T.sem.stored, 16)
+
+    g.wait_ge(T.sem.sent, left)
+    g.wait_ge(T.sem.stored, 16 * NCHUNK)

@@ -7,7 +7,7 @@ SCRATCH = {
     "land": ("dram", [NCHUNK, 128, COLS], "float32"),
 }
 SEMAPHORES = (["ld%d" % k for k in range(NCHUNK)]
-              + ["rel%d" % k for k in range(NCHUNK)]
+              + ["rel%d" % k for k in range(0, NCHUNK, 2)]
               + ["arr%d" % k for k in range(NCHUNK)]
               + ["sent", "stored"])
 

NCHUNK = 4
ROWS = 128 // NCHUNK
COLS = 1024 // (128 // ROWS)

SCRATCH = {
    "stage": ("dram", [NCHUNK, 128, COLS], "float32"),
    "land": ("dram", [NCHUNK, 128, COLS], "float32"),
}
SEMAPHORES = (["ld%d" % k for k in range(NCHUNK)]
              + ["rel%d" % k for k in range(0, NCHUNK, 2)]
              + ["arr%d" % k for k in range(NCHUNK)]
              + ["sent", "stored"])


def _engines(mask):
    return bin(mask).count("1")


def _helper(topo, src, dst):
    base = src - src % 8
    for c in range(base + 7, base - 1, -1):
        if topo.die(c) != topo.die(src) and topo.may_write(c, dst):
            return c
    return None


def rank_program(g, core, T, topo):
    routes = [(T.cores[s], T.cores[d]) for s, d in T.tables["PERM"]]
    rank = T.rank_of(core)

    if rank is None:
        for src, dst in routes:
            if _helper(topo, src, dst) != core:
                continue
            rid, pid = topo.addr(dst, core)
            mask = topo.mask(core, dst)
            left = 0
            for k in range(0, NCHUNK, 2):
                g.wait_ge(T.sem["rel%d" % k], _engines(topo.mask(src, core)))
                g.remote_dma(T.land[k], T.stage[k], T.sem["arr%d" % k], T.sem.sent, pid, rid, mask)
                left += _engines(mask)
            g.wait_ge(T.sem.sent, left)
        return

    dst = [d for s, d in routes if s == core][0]
    src = [s for s, d in routes if d == core][0]
    helper = _helper(topo, core, dst)

    for k in range(NCHUNK):
        g.sync.dma_start(T.stage[k], T.x[k * ROWS:(k + 1) * ROWS, :]).then_inc(T.sem["ld%d" % k], 16)

    left = 0
    for k in range(NCHUNK):
        g.wait_ge(T.sem["ld%d" % k], 16)
        if k % 2 == 0:
            to, out, sem = helper, T.stage[k], T.sem["rel%d" % k]
        else:
            to, out, sem = dst, T.land[k], T.sem["arr%d" % k]
        rid, pid = topo.addr(to, core)
        mask = topo.mask(core, to)
        g.remote_dma(out, T.stage[k], sem, T.sem.sent, pid, rid, mask)
        left += _engines(mask)

    for k in range(NCHUNK):
        q = g.sync if k % 2 == 0 else g.scalar
        frm = _helper(topo, src, core) if k % 2 == 0 else src
        q.wait_ge(T.sem["arr%d" % k], _engines(topo.mask(frm, core)))
        q.dma_start(T.y[k * ROWS:(k + 1) * ROWS, :], T.land[k]).then_inc(T.sem.stored, 16)

    g.wait_ge(T.sem.sent, left)
    g.wait_ge(T.sem.stored, 16 * NCHUNK)
